import numpy as np
import ml_dtypes


def mxq(x, axis, fmt="e4m3"):
    dtype, down = {"e4m3": (ml_dtypes.float8_e4m3fn, 7), "e5m2": (ml_dtypes.float8_e5m2, 14)}[fmt]
    v = np.moveaxis(np.asarray(x, np.float32).astype(ml_dtypes.bfloat16).astype(np.float64), axis, -1)
    blocks = v.reshape(v.shape[:-1] + (-1, 32))
    amax = np.abs(blocks).max(-1, keepdims=True)
    byte = np.maximum(np.where(amax > 0, np.frexp(amax)[1] - 1 + 127, 0) - down, 1)
    scale = np.exp2(byte - 127.0)
    codes = (blocks / scale).astype(np.float32).astype(dtype).astype(np.float64)
    return np.moveaxis((codes * scale).reshape(v.shape), -1, axis)


WIDE = False


def mx_kscale(k):
    if not WIDE:
        return np.ones(k)
    levels = np.array([10, -10, 5, -5, 0])
    if k % 512:
        return np.exp2(np.random.permutation(np.resize(levels, k // 32))).repeat(32)
    a = np.empty((k // 512, 16))
    for p in range(k // 512):
        a[p, :8] = np.random.permutation(np.resize(levels, 8))
        for g in range(8):
            far = levels[np.abs(levels - a[p, g]) >= 10]
            a[p, g + 8] = far[np.random.randint(len(far))]
    return np.exp2(a.ravel()).repeat(32)


def f64(x):
    return np.asarray(x).astype(np.float64)


def striped(idx):
    return np.tile(np.asarray(idx).reshape(-1, 16).T, (8, 1)).astype(np.uint16)


def unstriped(offs):
    return offs[:16].T.reshape(-1).astype(np.int64)


E2M1 = np.array([0.0, 0.5, 1.0, 1.5, 2.0, 3.0, 4.0, 6.0, -0.0, -0.5, -1.0, -1.5, -2.0, -3.0, -4.0, -6.0])


def pack_weight(w, fmt):
    k, n = w.shape
    w = f64(np.asarray(w, np.float32).astype(ml_dtypes.bfloat16)).reshape(k // 32, 32, n)
    amax = np.abs(w).max(1)
    if fmt == "e4m3":
        byte = np.frexp(amax)[1] - 1 + 127 - 7
    else:
        mant, ex = np.frexp(amax / 6.0)
        byte = np.where(mant > 0.5, ex, ex - 1) + 127
    byte = np.clip(np.where(amax > 0, byte, 1), 1, 254)
    scaled = (w * np.exp2(127.0 - byte)[:, None, :]).reshape(k, n).astype(np.float32)
    by_word = np.ascontiguousarray(scaled.reshape(k // 512, 128, 4, n).transpose(0, 1, 3, 2))
    if fmt == "e4m3":
        words = by_word.astype(ml_dtypes.float8_e4m3fn).view(np.uint8)
    else:
        c = by_word.astype(ml_dtypes.float4_e2m1fn).view(np.uint8) & 0xF
        words = (c[..., 0::2] | (c[..., 1::2] << 4)).reshape(k // 512, 128, 2 * n)
    return np.ascontiguousarray(words), np.ascontiguousarray(byte.astype(np.uint8).reshape(k // 512, 16, n))


def unpack_weight(words, scales, fmt):
    g, _, n = scales.shape
    words = np.ascontiguousarray(words).reshape(g, 128, n, -1)
    if fmt == "e4m3":
        vals = words.view(ml_dtypes.float8_e4m3fn).astype(np.float64)
    else:
        nib = np.empty((g, 128, n, 4), np.uint8)
        nib[..., 0::2] = words & 0xF
        nib[..., 1::2] = words >> 4
        vals = E2M1[nib]
    vals = vals * np.repeat(np.exp2(scales.astype(np.float64) - 127.0), 8, axis=1)[..., None]
    return vals.transpose(0, 1, 3, 2).reshape(g * 512, n)


def sigmoid(v):
    return 1.0 / (1.0 + np.exp(-v))


D, K, R, T, I, Q, G = 512, 512, 512, 2048, 512, 128, 32


def setup_inputs():
    n = np.random.standard_normal
    idx = np.random.permutation(T)[:I]
    fd = mx_kscale(D)
    fk = mx_kscale(K)
    fi = mx_kscale(I)
    keysp = pack_weight(n((D, T)) / fd[:, None], "e2m1")
    tabp = pack_weight(n((K, T)) / fk[:, None], "e2m1")
    return {
        "query": (n((D, Q)) * 0.6 / np.sqrt(D) * fd[:, None]).astype(np.float32),
        "query2": (n((D, Q)) * 1.0 / np.sqrt(D) * fd[:, None]).astype(np.float32),
        "keys_words": keysp[0],
        "keys_scales": keysp[1],
        "tab_words": tabp[0],
        "tab_scales": tabp[1],
        "w1": (n((K, R)) * 1 / np.sqrt(K) * fk[:, None]).astype(np.float32),
        "share": (np.random.uniform(0.4, 1.0, (R, 1))).astype(np.float32),
        "os": (np.random.uniform(4.0, 16.0, (1, I)) * fi).astype(np.float32),
        "vs": (np.random.uniform(0.5, 2.0, (1, I)) / fi).astype(np.float32),
        "offs": striped(idx),
    }


def reference(query, query2, keys_words, keys_scales, tab_words, tab_scales, w1, share, os, vs, offs):
    idx = unstriped(offs)
    keysu = unpack_weight(keys_words, keys_scales, "e2m1")
    tabu = unpack_weight(tab_words, tab_scales, "e2m1")
    queryq = mxq(f64(query), 0, "e4m3")
    keysidxg = keysu[:, idx]
    a = queryq.T @ keysidxg
    query2q = mxq(f64(query2), 0, "e4m3")
    b = query2q.T @ keysidxg
    p = np.exp(a - np.max(a, axis=1, keepdims=True)) * sigmoid(b)
    z = np.sum(p, axis=1, keepdims=True)
    w = p / z
    w1q = mxq(f64(w1), 0, "e4m3")
    tabidxg = tabu[:, idx]
    zh = w1q.T @ tabidxg
    mz = zh.reshape(R, G, I // G).mean(axis=2)
    mzr = np.repeat(mz, I // G, axis=1)
    hv = np.tanh(zh - mzr * f64(share))
    wo1 = w * f64(os)
    wt1 = wo1.T
    hw = hv * f64(vs)
    ht1 = hw.T
    wt1q = mxq(wt1, 0, "e4m3")
    ht1q = mxq(ht1, 0, "e4m3")
    o = wt1q.T @ ht1q
    return o

@@ -1,0 +1,205 @@
+from contextlib import ExitStack
+
+import concourse.mybir as mybir
+from concourse.masks import make_identity
+
+F32 = mybir.dt.float32
+BF16 = mybir.dt.bfloat16
+I32 = mybir.dt.int32
+U32 = mybir.dt.uint32
+U16 = mybir.dt.uint16
+U8 = mybir.dt.uint8
+FP8X4 = mybir.dt.float8_e4m3fn_x4
+FP4X4 = mybir.dt.float4_e2m1fn_x4
+ALU = mybir.AluOpType
+ACT = mybir.ActivationFunctionType
+AXIS = mybir.AxisListType
+
+FLOPS = 469762048
+
+P = 128
+PACK = 4
+POOL = 2048
+SLOTS = 512
+HIDDEN = 512
+BLOCKS = HIDDEN // P
+PAGE = 16
+PAGES = SLOTS // PAGE
+
+
+def tile_attend_lrcentred_asked_kernel(tc, query, query2, keys_words, keys_scales, tab_words, tab_scales, w1, share, slot_factor, value_scale, offs, out):
+    nc = tc.nc
+    with ExitStack() as ctx:
+        sb = ctx.enter_context(tc.tile_pool(name="sb", bufs=1))
+        ps = ctx.enter_context(tc.psum_pool(name="ps", bufs=1))
+
+        def tile(name, shape, dtype, tag=None):
+            return sb.tile(shape, dtype, name=name, tag=tag or name, align_bytes=64)
+
+        def bank(number, shape):
+            return ps.tile(shape, F32, name="bank%d" % number)
+
+        offsets = tile("offsets", [P, SLOTS // 16], U16)
+        nc.sync.dma_start(offsets[:], offs)
+
+        def load_words(name, words):
+            pool_words = tile(name, [P, POOL], U16)
+            nc.sync.dma_start(pool_words[:].bitcast(I32), words[0].bitcast(I32))
+            return pool_words
+
+        def load_scales(name, scales):
+            pool_scales = tile(name, [P, POOL], U8)
+            nc.gpsimd.memset(pool_scales[:].bitcast(I32), 0)
+            rows = scales[0].bitcast(I32).rearrange("(q f) n -> f q n", f=4)
+            for f in range(4):
+                nc.sync.dma_start(pool_scales[f:P:32, :].bitcast(I32), rows[f])
+            return pool_scales
+
+        def load_rows(name, src):
+            raw = tile(name, [P, PACK, src.shape[1]], F32)
+            nc.sync.dma_start(raw[:], src.rearrange("(p t) c -> p t c", t=PACK))
+            return raw
+
+        def gather(name, window, dtype, tag=None):
+            picked = tile(name, [P, SLOTS], dtype, tag)
+            nc.vector.tensor_copy(picked[:], window[:].indirect(offsets[:]))
+            return picked
+
+        def interleave(grouped, raw_cols):
+            nc.scalar.activation(
+                grouped.rearrange("p (c i) t -> p c t i", i=4),
+                raw_cols.rearrange("p t (c i) -> p c t i", i=4),
+                ACT.Copy,
+            )
+
+        def quantize(name, grouped, tag=None):
+            codes = tile(name + "_codes", [P, grouped.shape[1]], U32, tag)
+            scales = tile(name + "_scales", [P, grouped.shape[1]], U8)
+            nc.vector.quantize_mx(codes[:].bitcast(FP8X4), scales[:], grouped[:].rearrange("p c t -> p (c t)"))
+            return codes, scales
+
+        def product(dst, stationary, block, moving, moving_dtype):
+            cols = slice(block * P, (block + 1) * P)
+            nc.tensor.matmul_mx(
+                dst,
+                lhsT=stationary[0][:, cols].bitcast(FP8X4),
+                lhsT_scale=stationary[1][:, cols],
+                rhs=moving[0][:].bitcast(moving_dtype),
+                rhs_scale=moving[1][:],
+                start=True,
+                stop=True,
+            )
+
+        keys_pool_words = load_words("keys_pool_words", keys_words)
+        keys_pool_scales = load_scales("keys_pool_scales", keys_scales)
+        q2_raw = load_rows("q2_raw", query2)
+        q_raw = load_rows("q_raw", query)
+        tab_pool_words = load_words("tab_pool_words", tab_words)
+        tab_pool_scales = load_scales("tab_pool_scales", tab_scales)
+        w_lo = load_rows("w_lo", w1[:, 0 : 2 * P])
+        share_cols = tile("share_cols", [P, BLOCKS], F32)
+        with nc.allow_non_contiguous_dma(reason="one share a partition"):
+            nc.sync.dma_start(share_cols[:], share.rearrange("(j p) o -> p (j o)", p=P))
+        w_hi = load_rows("w_hi", w1[:, 2 * P : 4 * P])
+        vs_cols = tile("vs_cols", [P, PACK], F32)
+        nc.sync.dma_start(vs_cols[:], value_scale.rearrange("o (p t) -> p (o t)", t=PACK))
+
+        warm_in = tile("warm_in", [P, 1], F32)
+        nc.vector.memset(warm_in[:], 0.0)
+        warm_out = tile("warm_out", [P, 1], F32)
+        nc.scalar.activation(warm_out[:], warm_in[:], ACT.Sigmoid)
+
+        ident = tile("ident", [P, P], F32)
+        make_identity(nc, ident[:])
+        os_cols = tile("os_cols", [P, PACK], F32)
+        nc.gpsimd.dma_start(os_cols[:], slot_factor.rearrange("o (p t) -> p (o t)", t=PACK))
+        shift_factor = tile("shift_factor", [P, BLOCKS], F32)
+        nc.gpsimd.tensor_scalar(shift_factor[:], share_cols[:], -1.0 / PAGE, 0.0, ALU.mult, ALU.add)
+
+        def layer(j, w_mx, tab):
+            zh = bank(j, [P, SLOTS])
+            product(zh[:], w_mx, j % 2, tab, FP4X4)
+            sums = tile("sums%d" % j, [P, PAGES], F32)
+            nc.vector.tensor_reduce(sums[:], zh[:].rearrange("r (g u) -> r g u", u=PAGE), AXIS.X, ALU.add)
+            dealt = tile("dealt%d" % j, [P, PACK, P], F32)
+            nc.scalar.copy(dealt[:], zh[:].rearrange("r (p t) -> r t p", t=PACK))
+            shift = tile("shift%d" % j, [P, PAGES, 4], F32)
+            nc.scalar.activation(shift[:], sums[:].unsqueeze(2).to_broadcast([P, PAGES, 4]), ACT.Copy, scale=shift_factor[:, j : j + 1])
+            turned = bank((4, 6, 0, 1)[j], [P, PACK, P])
+            for t in range(PACK):
+                nc.tensor.matmul(turned[:, t, :], dealt[:, t, :], ident[:], start=True, stop=False, is_transpose=True)
+                nc.tensor.matmul(
+                    turned[:, t, :], shift[:].rearrange("r g c -> r (g c)"), ident[:], start=False, stop=True, is_transpose=True
+                )
+            return turned
+
+        def squash(j, turned):
+            hv = tile("hv%d" % j, [P, P, PACK], F32)
+            nc.scalar.activation(hv[:], turned[:].rearrange("p t r -> p r t"), ACT.Tanh)
+            return hv
+
+        def scale_values(j, hv):
+            hw = tile("hw%d" % j, [P, P, PACK], BF16)
+            nc.vector.tensor_tensor(hw[:], hv[:], vs_cols[:].unsqueeze(1).to_broadcast([P, P, PACK]), ALU.mult)
+            return hw
+
+        keys = (gather("keys_words_g", keys_pool_words, U16), gather("keys_scales_g", keys_pool_scales, U8))
+        qg = tile("qg", [P, 2 * P, PACK], BF16)
+        interleave(qg[:, 0:P, :], q2_raw[:])
+        interleave(qg[:, P : 2 * P, :], q_raw[:])
+        q_mx = quantize("q", qg)
+        b = bank(6, [P, SLOTS])
+        product(b[:], q_mx, 0, keys, FP4X4)
+        a = bank(5, [P, SLOTS])
+        product(a[:], q_mx, 1, keys, FP4X4)
+        os_rows = bank(7, [P, PACK, P])
+        for t in range(PACK):
+            nc.tensor.transpose(os_rows[:, t, :], os_cols[:, t : t + 1].to_broadcast([P, P]), ident[:])
+        gate = tile("gate", [P, SLOTS], F32)
+        nc.scalar.activation(gate[:], b[:], ACT.Sigmoid)
+        tab = (gather("tab_words_g", tab_pool_words, U16), gather("tab_scales_g", tab_pool_scales, U8))
+        wg_lo = tile("wg_lo", [P, 2 * P, PACK], BF16)
+        nc.gpsimd.tensor_scalar(
+            wg_lo[:], w_lo[:].rearrange("p t c -> p c t"), 1.0, 0.0, ALU.mult, ALU.add
+        )
+        neg_max = tile("neg_max", [P, 1], F32, "tab_pool_scales")
+        nc.vector.tensor_reduce(neg_max[:], a[:], AXIS.X, ALU.max, negate=True)
+        w_lo_mx = quantize("w_lo", wg_lo)
+        e = tile("e", [P, SLOTS], F32)
+        nc.scalar.activation(e[:], a[:], ACT.Exp, bias=neg_max[:])
+        wg_hi = tile("wg_hi", [P, 2 * P, PACK], BF16)
+        interleave(wg_hi[:], w_hi[:])
+        w_hi_mx = quantize("w_hi", wg_hi)
+        turned = [layer(j, w_lo_mx, tab) for j in range(2)]
+        p = tile("p", [P, SLOTS], F32)
+        z = tile("z", [P, 1], F32)
+        nc.vector.scalar_tensor_tensor(p[:], e[:], 1.0, gate[:], ALU.mult, ALU.mult, accum_out=z[:])
+        turned.append(layer(2, w_hi_mx, tab))
+        hv = [squash(0, turned[0])]
+        rz = tile("rz", [P, 1], F32)
+        nc.vector.reciprocal(rz[:], z[:])
+        turned.append(layer(3, w_hi_mx, tab))
+        hv.append(squash(1, turned[1]))
+        wo = tile("wo", [P, P, PACK], BF16)
+        nc.vector.scalar_tensor_tensor(wo[:], p[:].rearrange("q (p t) -> q p t", t=PACK), rz[:], os_rows[:].rearrange("q t p -> q p t"), ALU.mult, ALU.mult)
+        pairs = wo[:].rearrange("q p t -> q (p t)").bitcast(F32)
+        turned_pairs = bank(5, [P, 2, P])
+        for u in range(2):
+            nc.tensor.transpose(turned_pairs[:, u, :], pairs[:, u : 2 * P : 2], ident[:])
+        wt = tile("wt", [P, P, PACK], BF16)
+        nc.scalar.copy(
+            wt[:].rearrange("p q t -> p (q t)").bitcast(F32).rearrange("p (q u) -> p q u", u=2),
+            turned_pairs[:].rearrange("p u q -> p q u"),
+        )
+        wt_mx = quantize("wt", wt)
+        hv = hv + [squash(j, turned[j]) for j in range(2, BLOCKS)]
+        h_mx = [quantize("h%d" % j, scale_values(j, hv[j])) for j in range(BLOCKS)]
+        for j in range(BLOCKS):
+            acc = bank((2, 3, 4, 7)[j], [P, P])
+            product(acc[:], wt_mx, 0, h_mx[j], FP8X4)
+            result = tile("result%d" % j, [P, P], F32)
+            if j == BLOCKS - 1:
+                nc.vector.tensor_copy(result[:], acc[:])
+            else:
+                nc.scalar.copy(result[:], acc[:])
+            nc.sync.dma_start(out[:, j * P : (j + 1) * P], result[:])

@@ -21,13 +21,24 @@ P = 128
 PACK = 4
 POOL = 2048
 SLOTS = 512
-HIDDEN = 512
-BLOCKS = HIDDEN // P
+BLOCKS = 4
 PAGE = 16
 PAGES = SLOTS // PAGE
+PAGE_ROWS = PAGE // PACK
+QUADRANT = 32
+RUN = 4
+
+LAYER_BANKS = (0, 1, 2, 3)
+SCORE_BANK = 5
+GATE_BANK = 6
+FACTOR_BANK = 7
+TURNED_BANKS = (4, GATE_BANK, 0, 1)
+OUT_BANKS = (2, 3, 4)
 
 
-def tile_attend_lrcentred_asked_kernel(tc, query, query2, keys_words, keys_scales, tab_words, tab_scales, w1, share, slot_factor, value_scale, offs, out):
+def tile_attend_lrcentred_asked_kernel(
+    tc, query, query2, keys_words, keys_scales, tab_words, tab_scales, w1, share, slot_factor, value_scale, offs, out
+):
     nc = tc.nc
     with ExitStack() as ctx:
         sb = ctx.enter_context(tc.tile_pool(name="sb", bufs=1))
@@ -39,9 +50,6 @@ def tile_attend_lrcentred_asked_kernel(tc, query, query2, keys_words, keys_scale
         def bank(number, shape):
             return ps.tile(shape, F32, name="bank%d" % number)
 
-        offsets = tile("offsets", [P, SLOTS // 16], U16)
-        nc.sync.dma_start(offsets[:], offs)
-
         def load_words(name, words):
             pool_words = tile(name, [P, POOL], U16)
             nc.sync.dma_start(pool_words[:].bitcast(I32), words[0].bitcast(I32))
@@ -52,7 +60,7 @@ def tile_attend_lrcentred_asked_kernel(tc, query, query2, keys_words, keys_scale
             nc.gpsimd.memset(pool_scales[:].bitcast(I32), 0)
             rows = scales[0].bitcast(I32).rearrange("(q f) n -> f q n", f=4)
             for f in range(4):
-                nc.sync.dma_start(pool_scales[f:P:32, :].bitcast(I32), rows[f])
+                nc.sync.dma_start(pool_scales[f:P:QUADRANT, :].bitcast(I32), rows[f])
             return pool_scales
 
         def load_rows(name, src):
@@ -60,26 +68,27 @@ def tile_attend_lrcentred_asked_kernel(tc, query, query2, keys_words, keys_scale
             nc.sync.dma_start(raw[:], src.rearrange("(p t) c -> p t c", t=PACK))
             return raw
 
+        def load_slot_columns(name, src):
+            cols = tile(name, [P, PACK], F32)
+            nc.sync.dma_start(cols[:], src.rearrange("o (p t) -> p (o t)", t=PACK))
+            return cols
+
         def gather(name, window, dtype, tag=None):
             picked = tile(name, [P, SLOTS], dtype, tag)
             nc.vector.tensor_copy(picked[:], window[:].indirect(offsets[:]))
             return picked
 
-        def interleave(grouped, raw_cols):
-            nc.scalar.activation(
-                grouped.rearrange("p (c i) t -> p c t i", i=4),
-                raw_cols.rearrange("p t (c i) -> p c t i", i=4),
-                ACT.Copy,
-            )
+        def interleave(copy, grouped, raw_cols):
+            copy(grouped.rearrange("p (c i) t -> p c t i", i=RUN), raw_cols.rearrange("p t (c i) -> p c t i", i=RUN))
 
-        def quantize(name, grouped, tag=None):
-            codes = tile(name + "_codes", [P, grouped.shape[1]], U32, tag)
+        def quantize(name, grouped):
+            codes = tile(name + "_codes", [P, grouped.shape[1]], U32)
             scales = tile(name + "_scales", [P, grouped.shape[1]], U8)
             nc.vector.quantize_mx(codes[:].bitcast(FP8X4), scales[:], grouped[:].rearrange("p c t -> p (c t)"))
             return codes, scales
 
-        def product(dst, stationary, block, moving, moving_dtype):
-            cols = slice(block * P, (block + 1) * P)
+        def product(dst, stationary, part, moving, moving_dtype):
+            cols = slice(part * P, (part + 1) * P)
             nc.tensor.matmul_mx(
                 dst,
                 lhsT=stationary[0][:, cols].bitcast(FP8X4),
@@ -90,47 +99,48 @@ def tile_attend_lrcentred_asked_kernel(tc, query, query2, keys_words, keys_scale
                 stop=True,
             )
 
+        offsets = tile("offsets", [P, SLOTS // 16], U16)
+        nc.sync.dma_start(offsets[:], offs)
         keys_pool_words = load_words("keys_pool_words", keys_words)
         keys_pool_scales = load_scales("keys_pool_scales", keys_scales)
         q2_raw = load_rows("q2_raw", query2)
         q_raw = load_rows("q_raw", query)
         tab_pool_words = load_words("tab_pool_words", tab_words)
         tab_pool_scales = load_scales("tab_pool_scales", tab_scales)
-        w_lo = load_rows("w_lo", w1[:, 0 : 2 * P])
+        w_raw = load_rows("w_raw", w1)
+        factor_cols = load_slot_columns("factor_cols", slot_factor)
         share_cols = tile("share_cols", [P, BLOCKS], F32)
-        with nc.allow_non_contiguous_dma(reason="one share a partition"):
-            nc.sync.dma_start(share_cols[:], share.rearrange("(j p) o -> p (j o)", p=P))
-        w_hi = load_rows("w_hi", w1[:, 2 * P : 4 * P])
-        vs_cols = tile("vs_cols", [P, PACK], F32)
-        nc.sync.dma_start(vs_cols[:], value_scale.rearrange("o (p t) -> p (o t)", t=PACK))
-
-        warm_in = tile("warm_in", [P, 1], F32)
-        nc.vector.memset(warm_in[:], 0.0)
-        warm_out = tile("warm_out", [P, 1], F32)
-        nc.scalar.activation(warm_out[:], warm_in[:], ACT.Sigmoid)
+        with nc.allow_non_contiguous_dma(reason="each partition takes one share for each block of hidden features"):
+            nc.sync.dma_start(share_cols[:], share.rearrange("(j r) o -> r (j o)", r=P))
+        scale_cols = load_slot_columns("scale_cols", value_scale)
 
         ident = tile("ident", [P, P], F32)
         make_identity(nc, ident[:])
-        os_cols = tile("os_cols", [P, PACK], F32)
-        nc.gpsimd.dma_start(os_cols[:], slot_factor.rearrange("o (p t) -> p (o t)", t=PACK))
         shift_factor = tile("shift_factor", [P, BLOCKS], F32)
         nc.gpsimd.tensor_scalar(shift_factor[:], share_cols[:], -1.0 / PAGE, 0.0, ALU.mult, ALU.add)
 
-        def layer(j, w_mx, tab):
-            zh = bank(j, [P, SLOTS])
+        def layer(j, w_mx):
+            zh = bank(LAYER_BANKS[j], [P, SLOTS])
             product(zh[:], w_mx, j % 2, tab, FP4X4)
             sums = tile("sums%d" % j, [P, PAGES], F32)
             nc.vector.tensor_reduce(sums[:], zh[:].rearrange("r (g u) -> r g u", u=PAGE), AXIS.X, ALU.add)
+            return zh, sums
+
+        def turn_adding_shift(j, zh, sums):
             dealt = tile("dealt%d" % j, [P, PACK, P], F32)
             nc.scalar.copy(dealt[:], zh[:].rearrange("r (p t) -> r t p", t=PACK))
-            shift = tile("shift%d" % j, [P, PAGES, 4], F32)
-            nc.scalar.activation(shift[:], sums[:].unsqueeze(2).to_broadcast([P, PAGES, 4]), ACT.Copy, scale=shift_factor[:, j : j + 1])
-            turned = bank((4, 6, 0, 1)[j], [P, PACK, P])
+            shift = tile("shift%d" % j, [P, PAGES, PAGE_ROWS], F32)
+            nc.scalar.activation(
+                shift[:],
+                sums[:].unsqueeze(2).to_broadcast([P, PAGES, PAGE_ROWS]),
+                ACT.Copy,
+                scale=shift_factor[:, j : j + 1],
+            )
+            shift_cols = shift[:].rearrange("r g c -> r (g c)")
+            turned = bank(TURNED_BANKS[j], [P, PACK, P])
             for t in range(PACK):
                 nc.tensor.matmul(turned[:, t, :], dealt[:, t, :], ident[:], start=True, stop=False, is_transpose=True)
-                nc.tensor.matmul(
-                    turned[:, t, :], shift[:].rearrange("r g c -> r (g c)"), ident[:], start=False, stop=True, is_transpose=True
-                )
+                nc.tensor.matmul(turned[:, t, :], shift_cols, ident[:], start=False, stop=True, is_transpose=True)
             return turned
 
         def squash(j, turned):
@@ -138,68 +148,96 @@ def tile_attend_lrcentred_asked_kernel(tc, query, query2, keys_words, keys_scale
             nc.scalar.activation(hv[:], turned[:].rearrange("p t r -> p r t"), ACT.Tanh)
             return hv
 
-        def scale_values(j, hv):
-            hw = tile("hw%d" % j, [P, P, PACK], BF16)
-            nc.vector.tensor_tensor(hw[:], hv[:], vs_cols[:].unsqueeze(1).to_broadcast([P, P, PACK]), ALU.mult)
-            return hw
-
         keys = (gather("keys_words_g", keys_pool_words, U16), gather("keys_scales_g", keys_pool_scales, U8))
-        qg = tile("qg", [P, 2 * P, PACK], BF16)
-        interleave(qg[:, 0:P, :], q2_raw[:])
-        interleave(qg[:, P : 2 * P, :], q_raw[:])
-        q_mx = quantize("q", qg)
-        b = bank(6, [P, SLOTS])
+        q_grouped = tile("q_grouped", [P, 2 * P, PACK], BF16)
+        interleave(nc.scalar.copy, q_grouped[:, 0:P, :], q2_raw[:])
+        interleave(nc.scalar.copy, q_grouped[:, P : 2 * P, :], q_raw[:])
+        q_mx = quantize("q", q_grouped)
+        b = bank(GATE_BANK, [P, SLOTS])
         product(b[:], q_mx, 0, keys, FP4X4)
-        a = bank(5, [P, SLOTS])
+        a = bank(SCORE_BANK, [P, SLOTS])
         product(a[:], q_mx, 1, keys, FP4X4)
-        os_rows = bank(7, [P, PACK, P])
+        factor_rows = bank(FACTOR_BANK, [P, PACK, P])
         for t in range(PACK):
-            nc.tensor.transpose(os_rows[:, t, :], os_cols[:, t : t + 1].to_broadcast([P, P]), ident[:])
+            nc.tensor.transpose(factor_rows[:, t, :], factor_cols[:, t : t + 1].to_broadcast([P, P]), ident[:])
         gate = tile("gate", [P, SLOTS], F32)
         nc.scalar.activation(gate[:], b[:], ACT.Sigmoid)
-        tab = (gather("tab_words_g", tab_pool_words, U16), gather("tab_scales_g", tab_pool_scales, U8))
-        wg_lo = tile("wg_lo", [P, 2 * P, PACK], BF16)
-        nc.gpsimd.tensor_scalar(
-            wg_lo[:], w_lo[:].rearrange("p t c -> p c t"), 1.0, 0.0, ALU.mult, ALU.add
-        )
-        neg_max = tile("neg_max", [P, 1], F32, "tab_pool_scales")
+
+        tab = (gather("tab_words_g", tab_pool_words, U16, "q_raw"), gather("tab_scales_g", tab_pool_scales, U8))
+        w_hi_grouped = tile("w_hi_grouped", [P, 2 * P, PACK], BF16)
+        interleave(nc.scalar.copy, w_hi_grouped[:], w_raw[:, :, 2 * P : 4 * P])
+        w_lo_grouped = tile("w_lo_grouped", [P, 2 * P, PACK], BF16)
+        interleave(nc.vector.tensor_copy, w_lo_grouped[:], w_raw[:, :, 0 : 2 * P])
+        w_lo_mx = quantize("w_lo", w_lo_grouped)
+        w_hi_mx = quantize("w_hi", w_hi_grouped)
+
+        neg_max = tile("neg_max", [P, 1], F32, "w_raw")
         nc.vector.tensor_reduce(neg_max[:], a[:], AXIS.X, ALU.max, negate=True)
-        w_lo_mx = quantize("w_lo", wg_lo)
         e = tile("e", [P, SLOTS], F32)
         nc.scalar.activation(e[:], a[:], ACT.Exp, bias=neg_max[:])
-        wg_hi = tile("wg_hi", [P, 2 * P, PACK], BF16)
-        interleave(wg_hi[:], w_hi[:])
-        w_hi_mx = quantize("w_hi", wg_hi)
-        turned = [layer(j, w_lo_mx, tab) for j in range(2)]
-        p = tile("p", [P, SLOTS], F32)
-        z = tile("z", [P, 1], F32)
-        nc.vector.scalar_tensor_tensor(p[:], e[:], 1.0, gate[:], ALU.mult, ALU.mult, accum_out=z[:])
-        turned.append(layer(2, w_hi_mx, tab))
+
+        groups = ((0, 1), (2,), (3,))
+        hw = [tile("hw%d" % g, [P, len(members) * P, PACK], BF16) for g, members in enumerate(groups)]
+
+        turned = [turn_adding_shift(j, *layer(j, w_mx)) for j, w_mx in enumerate((w_lo_mx, w_lo_mx, w_hi_mx))]
         hv = [squash(0, turned[0])]
-        rz = tile("rz", [P, 1], F32)
-        nc.vector.reciprocal(rz[:], z[:])
-        turned.append(layer(3, w_hi_mx, tab))
-        hv.append(squash(1, turned[1]))
+
+        gated = tile("gated", [P, SLOTS], F32)
+        z = tile("z", [P, 1], F32)
+        nc.vector.scalar_tensor_tensor(gated[:], e[:], 1.0, gate[:], ALU.mult, ALU.mult, accum_out=z[:])
+        last = BLOCKS - 1
+        last_zh, last_sums = layer(last, w_hi_mx)
+        z_inverse = tile("z_inverse", [P, 1], F32)
+        nc.vector.reciprocal(z_inverse[:], z[:])
+
+        last_dealt = tile("last_dealt", [P, PACK, P], F32)
+        nc.vector.scalar_tensor_tensor(
+            last_dealt[:].rearrange("r t p -> r p t"),
+            last_sums[:].unsqueeze(2).to_broadcast([P, PAGES, PAGE]),
+            shift_factor[:, last : last + 1],
+            last_zh[:].rearrange("r (g u) -> r g u", u=PAGE),
+            ALU.mult,
+            ALU.add,
+        )
+
         wo = tile("wo", [P, P, PACK], BF16)
-        nc.vector.scalar_tensor_tensor(wo[:], p[:].rearrange("q (p t) -> q p t", t=PACK), rz[:], os_rows[:].rearrange("q t p -> q p t"), ALU.mult, ALU.mult)
+        nc.vector.scalar_tensor_tensor(
+            wo[:],
+            gated[:].rearrange("q (p t) -> q p t", t=PACK),
+            z_inverse[:],
+            factor_rows[:].rearrange("q t p -> q p t"),
+            ALU.mult,
+            ALU.mult,
+        )
         pairs = wo[:].rearrange("q p t -> q (p t)").bitcast(F32)
-        turned_pairs = bank(5, [P, 2, P])
+        turned_pairs = bank(SCORE_BANK, [P, 2, P])
         for u in range(2):
             nc.tensor.transpose(turned_pairs[:, u, :], pairs[:, u : 2 * P : 2], ident[:])
+
+        turned.append(bank(TURNED_BANKS[last], [P, PACK, P]))
+        for t in range(PACK):
+            nc.tensor.transpose(turned[last][:, t, :], last_dealt[:, t, :], ident[:])
+        hv.append(squash(1, turned[1]))
+
         wt = tile("wt", [P, P, PACK], BF16)
         nc.scalar.copy(
             wt[:].rearrange("p q t -> p (q t)").bitcast(F32).rearrange("p (q u) -> p q u", u=2),
             turned_pairs[:].rearrange("p u q -> p q u"),
         )
         wt_mx = quantize("wt", wt)
-        hv = hv + [squash(j, turned[j]) for j in range(2, BLOCKS)]
-        h_mx = [quantize("h%d" % j, scale_values(j, hv[j])) for j in range(BLOCKS)]
-        for j in range(BLOCKS):
-            acc = bank((2, 3, 4, 7)[j], [P, P])
-            product(acc[:], wt_mx, 0, h_mx[j], FP8X4)
-            result = tile("result%d" % j, [P, P], F32)
-            if j == BLOCKS - 1:
-                nc.vector.tensor_copy(result[:], acc[:])
-            else:
-                nc.scalar.copy(result[:], acc[:])
-            nc.sync.dma_start(out[:, j * P : (j + 1) * P], result[:])
+        hv.extend(squash(j, turned[j]) for j in range(2, BLOCKS))
+
+        scale_rows = scale_cols[:].unsqueeze(1).to_broadcast([P, P, PACK])
+        h_mx = []
+        for g, members in enumerate(groups):
+            for place, j in enumerate(members):
+                nc.vector.tensor_tensor(hw[g][:, place * P : (place + 1) * P, :], hv[j][:], scale_rows, ALU.mult)
+            h_mx.append(quantize("h%d" % g, hw[g]))
+
+        for g, members in enumerate(groups):
+            acc = bank(OUT_BANKS[g], [P, len(members) * P])
+            product(acc[:], wt_mx, 0, h_mx[g], FP8X4)
+            result = tile("result%d" % g, [P, len(members) * P], F32)
+            copy_out = nc.vector.tensor_copy if last in members else nc.scalar.copy
+            copy_out(result[:], acc[:])
+            nc.sync.dma_start(out[:, members[0] * P : (members[-1] + 1) * P], result[:])

from contextlib import ExitStack

import concourse.mybir as mybir
from concourse.masks import make_identity

F32 = mybir.dt.float32
BF16 = mybir.dt.bfloat16
I32 = mybir.dt.int32
U32 = mybir.dt.uint32
U16 = mybir.dt.uint16
U8 = mybir.dt.uint8
FP8X4 = mybir.dt.float8_e4m3fn_x4
FP4X4 = mybir.dt.float4_e2m1fn_x4
ALU = mybir.AluOpType
ACT = mybir.ActivationFunctionType
AXIS = mybir.AxisListType

FLOPS = 469762048

P = 128
PACK = 4
POOL = 2048
SLOTS = 512
BLOCKS = 4
PAGE = 16
PAGES = SLOTS // PAGE
PAGE_ROWS = PAGE // PACK
QUADRANT = 32
RUN = 4

LAYER_BANKS = (0, 1, 2, 3)
SCORE_BANK = 5
GATE_BANK = 6
FACTOR_BANK = 7
TURNED_BANKS = (4, GATE_BANK, 0, 1)
OUT_BANKS = (2, 3, 4)


def tile_attend_lrcentred_asked_kernel(
    tc, query, query2, keys_words, keys_scales, tab_words, tab_scales, w1, share, slot_factor, value_scale, offs, out
):
    nc = tc.nc
    with ExitStack() as ctx:
        sb = ctx.enter_context(tc.tile_pool(name="sb", bufs=1))
        ps = ctx.enter_context(tc.psum_pool(name="ps", bufs=1))

        def tile(name, shape, dtype, tag=None):
            return sb.tile(shape, dtype, name=name, tag=tag or name, align_bytes=64)

        def bank(number, shape):
            return ps.tile(shape, F32, name="bank%d" % number)

        def load_words(name, words):
            pool_words = tile(name, [P, POOL], U16)
            nc.sync.dma_start(pool_words[:].bitcast(I32), words[0].bitcast(I32))
            return pool_words

        def load_scales(name, scales):
            pool_scales = tile(name, [P, POOL], U8)
            nc.gpsimd.memset(pool_scales[:].bitcast(I32), 0)
            rows = scales[0].bitcast(I32).rearrange("(q f) n -> f q n", f=4)
            for f in range(4):
                nc.sync.dma_start(pool_scales[f:P:QUADRANT, :].bitcast(I32), rows[f])
            return pool_scales

        def load_rows(name, src):
            raw = tile(name, [P, PACK, src.shape[1]], F32)
            nc.sync.dma_start(raw[:], src.rearrange("(p t) c -> p t c", t=PACK))
            return raw

        def load_slot_columns(name, src):
            cols = tile(name, [P, PACK], F32)
            nc.sync.dma_start(cols[:], src.rearrange("o (p t) -> p (o t)", t=PACK))
            return cols

        def gather(name, window, dtype, tag=None):
            picked = tile(name, [P, SLOTS], dtype, tag)
            nc.vector.tensor_copy(picked[:], window[:].indirect(offsets[:]))
            return picked

        def interleave(copy, grouped, raw_cols):
            copy(grouped.rearrange("p (c i) t -> p c t i", i=RUN), raw_cols.rearrange("p t (c i) -> p c t i", i=RUN))

        def quantize(name, grouped):
            codes = tile(name + "_codes", [P, grouped.shape[1]], U32)
            scales = tile(name + "_scales", [P, grouped.shape[1]], U8)
            nc.vector.quantize_mx(codes[:].bitcast(FP8X4), scales[:], grouped[:].rearrange("p c t -> p (c t)"))
            return codes, scales

        def product(dst, stationary, part, moving, moving_dtype):
            cols = slice(part * P, (part + 1) * P)
            nc.tensor.matmul_mx(
                dst,
                lhsT=stationary[0][:, cols].bitcast(FP8X4),
                lhsT_scale=stationary[1][:, cols],
                rhs=moving[0][:].bitcast(moving_dtype),
                rhs_scale=moving[1][:],
                start=True,
                stop=True,
            )

        offsets = tile("offsets", [P, SLOTS // 16], U16)
        nc.sync.dma_start(offsets[:], offs)
        keys_pool_words = load_words("keys_pool_words", keys_words)
        keys_pool_scales = load_scales("keys_pool_scales", keys_scales)
        q2_raw = load_rows("q2_raw", query2)
        q_raw = load_rows("q_raw", query)
        tab_pool_words = load_words("tab_pool_words", tab_words)
        tab_pool_scales = load_scales("tab_pool_scales", tab_scales)
        w_raw = load_rows("w_raw", w1)
        factor_cols = load_slot_columns("factor_cols", slot_factor)
        share_cols = tile("share_cols", [P, BLOCKS], F32)
        with nc.allow_non_contiguous_dma(reason="each partition takes one share for each block of hidden features"):
            nc.sync.dma_start(share_cols[:], share.rearrange("(j r) o -> r (j o)", r=P))
        scale_cols = load_slot_columns("scale_cols", value_scale)

        ident = tile("ident", [P, P], F32)
        make_identity(nc, ident[:])
        shift_factor = tile("shift_factor", [P, BLOCKS], F32)
        nc.gpsimd.tensor_scalar(shift_factor[:], share_cols[:], -1.0 / PAGE, 0.0, ALU.mult, ALU.add)

        def layer(j, w_mx):
            zh = bank(LAYER_BANKS[j], [P, SLOTS])
            product(zh[:], w_mx, j % 2, tab, FP4X4)
            sums = tile("sums%d" % j, [P, PAGES], F32)
            nc.vector.tensor_reduce(sums[:], zh[:].rearrange("r (g u) -> r g u", u=PAGE), AXIS.X, ALU.add)
            return zh, sums

        def turn_adding_shift(j, zh, sums):
            dealt = tile("dealt%d" % j, [P, PACK, P], F32)
            nc.scalar.copy(dealt[:], zh[:].rearrange("r (p t) -> r t p", t=PACK))
            shift = tile("shift%d" % j, [P, PAGES, PAGE_ROWS], F32)
            nc.scalar.activation(
                shift[:],
                sums[:].unsqueeze(2).to_broadcast([P, PAGES, PAGE_ROWS]),
                ACT.Copy,
                scale=shift_factor[:, j : j + 1],
            )
            shift_cols = shift[:].rearrange("r g c -> r (g c)")
            turned = bank(TURNED_BANKS[j], [P, PACK, P])
            for t in range(PACK):
                nc.tensor.matmul(turned[:, t, :], dealt[:, t, :], ident[:], start=True, stop=False, is_transpose=True)
                nc.tensor.matmul(turned[:, t, :], shift_cols, ident[:], start=False, stop=True, is_transpose=True)
            return turned

        def squash(j, turned):
            hv = tile("hv%d" % j, [P, P, PACK], F32)
            nc.scalar.activation(hv[:], turned[:].rearrange("p t r -> p r t"), ACT.Tanh)
            return hv

        keys = (gather("keys_words_g", keys_pool_words, U16), gather("keys_scales_g", keys_pool_scales, U8))
        q_grouped = tile("q_grouped", [P, 2 * P, PACK], BF16)
        interleave(nc.scalar.copy, q_grouped[:, 0:P, :], q2_raw[:])
        interleave(nc.scalar.copy, q_grouped[:, P : 2 * P, :], q_raw[:])
        q_mx = quantize("q", q_grouped)
        b = bank(GATE_BANK, [P, SLOTS])
        product(b[:], q_mx, 0, keys, FP4X4)
        a = bank(SCORE_BANK, [P, SLOTS])
        product(a[:], q_mx, 1, keys, FP4X4)
        factor_rows = bank(FACTOR_BANK, [P, PACK, P])
        for t in range(PACK):
            nc.tensor.transpose(factor_rows[:, t, :], factor_cols[:, t : t + 1].to_broadcast([P, P]), ident[:])
        gate = tile("gate", [P, SLOTS], F32)
        nc.scalar.activation(gate[:], b[:], ACT.Sigmoid)

        tab = (gather("tab_words_g", tab_pool_words, U16, "q_raw"), gather("tab_scales_g", tab_pool_scales, U8))
        w_hi_grouped = tile("w_hi_grouped", [P, 2 * P, PACK], BF16)
        interleave(nc.scalar.copy, w_hi_grouped[:], w_raw[:, :, 2 * P : 4 * P])
        w_lo_grouped = tile("w_lo_grouped", [P, 2 * P, PACK], BF16)
        interleave(nc.vector.tensor_copy, w_lo_grouped[:], w_raw[:, :, 0 : 2 * P])
        w_lo_mx = quantize("w_lo", w_lo_grouped)
        w_hi_mx = quantize("w_hi", w_hi_grouped)

        neg_max = tile("neg_max", [P, 1], F32, "w_raw")
        nc.vector.tensor_reduce(neg_max[:], a[:], AXIS.X, ALU.max, negate=True)
        e = tile("e", [P, SLOTS], F32)
        nc.scalar.activation(e[:], a[:], ACT.Exp, bias=neg_max[:])

        groups = ((0, 1), (2,), (3,))
        hw = [tile("hw%d" % g, [P, len(members) * P, PACK], BF16) for g, members in enumerate(groups)]

        turned = [turn_adding_shift(j, *layer(j, w_mx)) for j, w_mx in enumerate((w_lo_mx, w_lo_mx, w_hi_mx))]
        hv = [squash(0, turned[0])]

        gated = tile("gated", [P, SLOTS], F32)
        z = tile("z", [P, 1], F32)
        nc.vector.scalar_tensor_tensor(gated[:], e[:], 1.0, gate[:], ALU.mult, ALU.mult, accum_out=z[:])
        last = BLOCKS - 1
        last_zh, last_sums = layer(last, w_hi_mx)
        z_inverse = tile("z_inverse", [P, 1], F32)
        nc.vector.reciprocal(z_inverse[:], z[:])

        last_dealt = tile("last_dealt", [P, PACK, P], F32)
        nc.vector.scalar_tensor_tensor(
            last_dealt[:].rearrange("r t p -> r p t"),
            last_sums[:].unsqueeze(2).to_broadcast([P, PAGES, PAGE]),
            shift_factor[:, last : last + 1],
            last_zh[:].rearrange("r (g u) -> r g u", u=PAGE),
            ALU.mult,
            ALU.add,
        )

        wo = tile("wo", [P, P, PACK], BF16)
        nc.vector.scalar_tensor_tensor(
            wo[:],
            gated[:].rearrange("q (p t) -> q p t", t=PACK),
            z_inverse[:],
            factor_rows[:].rearrange("q t p -> q p t"),
            ALU.mult,
            ALU.mult,
        )
        pairs = wo[:].rearrange("q p t -> q (p t)").bitcast(F32)
        turned_pairs = bank(SCORE_BANK, [P, 2, P])
        for u in range(2):
            nc.tensor.transpose(turned_pairs[:, u, :], pairs[:, u : 2 * P : 2], ident[:])

        turned.append(bank(TURNED_BANKS[last], [P, PACK, P]))
        for t in range(PACK):
            nc.tensor.transpose(turned[last][:, t, :], last_dealt[:, t, :], ident[:])
        hv.append(squash(1, turned[1]))

        wt = tile("wt", [P, P, PACK], BF16)
        nc.scalar.copy(
            wt[:].rearrange("p q t -> p (q t)").bitcast(F32).rearrange("p (q u) -> p q u", u=2),
            turned_pairs[:].rearrange("p u q -> p q u"),
        )
        wt_mx = quantize("wt", wt)
        hv.extend(squash(j, turned[j]) for j in range(2, BLOCKS))

        scale_rows = scale_cols[:].unsqueeze(1).to_broadcast([P, P, PACK])
        h_mx = []
        for g, members in enumerate(groups):
            for place, j in enumerate(members):
                nc.vector.tensor_tensor(hw[g][:, place * P : (place + 1) * P, :], hv[j][:], scale_rows, ALU.mult)
            h_mx.append(quantize("h%d" % g, hw[g]))

        for g, members in enumerate(groups):
            acc = bank(OUT_BANKS[g], [P, len(members) * P])
            product(acc[:], wt_mx, 0, h_mx[g], FP8X4)
            result = tile("result%d" % g, [P, len(members) * P], F32)
            copy_out = nc.vector.tensor_copy if last in members else nc.scalar.copy
            copy_out(result[:], acc[:])
            nc.sync.dma_start(out[:, members[0] * P : (members[-1] + 1) * P], result[:])
